import numpy as np
import ml_dtypes


def mxq(x, axis, fmt="e4m3"):
    dtype, down = {"e4m3": (ml_dtypes.float8_e4m3fn, 7), "e5m2": (ml_dtypes.float8_e5m2, 14)}[fmt]
    v = np.moveaxis(np.asarray(x, np.float32).astype(ml_dtypes.bfloat16).astype(np.float64), axis, -1)
    blocks = v.reshape(v.shape[:-1] + (-1, 32))
    amax = np.abs(blocks).max(-1, keepdims=True)
    byte = np.maximum(np.where(amax > 0, np.frexp(amax)[1] - 1 + 127, 0) - down, 1)
    scale = np.exp2(byte - 127.0)
    codes = (blocks / scale).astype(np.float32).astype(dtype).astype(np.float64)
    return np.moveaxis((codes * scale).reshape(v.shape), -1, axis)


WIDE = False


def mx_kscale(k):
    if not WIDE:
        return np.ones(k)
    levels = np.array([10, -10, 5, -5, 0])
    if k % 512:
        return np.exp2(np.random.permutation(np.resize(levels, k // 32))).repeat(32)
    a = np.empty((k // 512, 16))
    for p in range(k // 512):
        a[p, :8] = np.random.permutation(np.resize(levels, 8))
        for g in range(8):
            far = levels[np.abs(levels - a[p, g]) >= 10]
            a[p, g + 8] = far[np.random.randint(len(far))]
    return np.exp2(a.ravel()).repeat(32)


def f64(x):
    return np.asarray(x).astype(np.float64)


def striped(idx):
    return np.tile(idx.reshape(-1, 16).T, (8, 1)).astype(np.uint16)


def unstriped(offs):
    return offs[:16].T.reshape(-1).astype(np.int64)


def striped8(idx):
    return np.concatenate([x.reshape(-1, 16).T for x in idx]).astype(np.uint16)


def runs(offs, k):
    lists = np.stack([offs[16 * r : 16 * r + 16].T.reshape(-1) for r in range(8)]).astype(np.int64)
    return lists[np.arange(k) % 512 // 64]


def pack_weight(w):
    k, n = w.shape
    w = f64(np.asarray(w, np.float32).astype(ml_dtypes.bfloat16)).reshape(k // 32, 32, n)
    amax = np.abs(w).max(1)
    byte = np.clip(np.where(amax > 0, np.frexp(amax)[1] - 1 + 127 - 7, 1), 1, 254)
    scaled = (w * np.exp2(127.0 - byte)[:, None, :]).reshape(k, n).astype(np.float32)
    words = np.ascontiguousarray(scaled.reshape(k // 512, 128, 4, n).transpose(0, 1, 3, 2)).astype(ml_dtypes.float8_e4m3fn).view(np.uint8)
    return words, np.ascontiguousarray(byte.astype(np.uint8).reshape(k // 512, 16, n))


def unpack_weight(words, scales):
    g, p, n, _ = words.shape
    vals = np.ascontiguousarray(words).view(ml_dtypes.float8_e4m3fn).astype(np.float64) * np.repeat(np.exp2(scales.astype(np.float64) - 127.0), 8, axis=1)[..., None]
    return vals.transpose(0, 1, 3, 2).reshape(g * 512, n)


def sigmoid(v):
    return 1.0 / (1.0 + np.exp(-np.maximum(v, -700.0)))


K, T, S, V, G, H, J = 512, 1024, 512, 512, 2048, 512, 512


def setup_inputs():
    n = np.random.standard_normal
    s = mx_kscale(K)[:, None]
    u = mx_kscale(S)
    packed_xT = pack_weight(n((K, T)) * s)
    packed_dT = pack_weight(n((K, G)) / s)
    return {
        "x_words": packed_xT[0],
        "x_scales": packed_xT[1],
        "d_words": packed_dT[0],
        "d_scales": packed_dT[1],
        "w1": (n((K, H)) / np.sqrt(K) / s).astype(np.float32),
        "tab": n((H, J)).astype(np.float32),
        "ga": (np.random.uniform(0.5, 1.5, (H, 1)) * u[:, None]).astype(np.float32),
        "gb": (np.random.uniform(0.5, 1.5, (H, 1)) / u[:, None]).astype(np.float32),
        "tab2": np.random.uniform(0.4, 1.4, (S, J)).astype(np.float32),
        "offs": striped(np.random.permutation(T)[:S]),
        "k1": striped8(np.random.randint(0, G, (8, H))),
        "two": striped(np.random.permutation(T)[:V]),
        "n1": striped8(np.stack([np.random.permutation(S) for _ in range(8)])),
        "n2": striped8(np.stack([np.random.permutation(S) for _ in range(8)])),
        "n3": striped8(np.random.randint(0, J, (8, V))),
        "n4": striped8(np.stack([np.random.permutation(V) for _ in range(8)])),
        "n5": striped8(np.random.randint(0, J, (8, V))),
        "n6": striped8(np.stack([np.random.permutation(V) for _ in range(8)])),
    }


def reference(x_words, x_scales, d_words, d_scales, w1, tab, ga, gb, tab2, offs, k1, two, n1, n2, n3, n4, n5, n6):
    d_k1 = unpack_weight(d_words, d_scales)[np.arange(K)[:, None], runs(k1, K)]
    xq = unpack_weight(x_words, x_scales)[:, unstriped(offs)]
    a = 0.0625 * (d_k1.T @ xq)
    st = a[np.arange(H)[:, None], runs(n1, H)] - a
    z = f64(ga) * (a * (sigmoid(st[np.arange(H)[:, None], runs(n2, H)])))
    x_two = unpack_weight(x_words, x_scales)[:, unstriped(two)]
    b = mxq(f64(w1), 0, "e4m3").T @ x_two
    z2 = f64(gb) * (np.maximum(b + f64(tab)[np.arange(H)[:, None], runs(n3, H)], b[np.arange(H)[:, None], runs(n4, H)]))
    s = 0.0625 * ((mxq(z, 0, "e4m3").T @ mxq(z2, 0, "e4m3")))
    return s * (f64(tab2)[np.arange(S)[:, None], runs(n5, S)]) - (0.5 * (s[np.arange(S)[:, None], runs(n6, S)]))

@@ -1,0 +1,207 @@
+from contextlib import ExitStack
+
+import concourse.mybir as mybir
+
+F32 = mybir.dt.float32
+BF16 = mybir.dt.bfloat16
+I32 = mybir.dt.int32
+U32 = mybir.dt.uint32
+U16 = mybir.dt.uint16
+U8 = mybir.dt.uint8
+FP8X4 = mybir.dt.float8_e4m3fn_x4
+ALU = mybir.AluOpType
+ACT = mybir.ActivationFunctionType
+
+P = 128
+PACK = 4
+W = 512
+HALF = 256
+T = 1024
+G = 2048
+FLOPS = 3 * 2 * 512 * 512 * 512
+
+
+def tile_picked_ckqhopdkindkindg_none_p_kernel(
+    tc, x_words, x_scales, d_words, d_scales, w1, tab, ga, gb, tab2, offs, k1, two, n1, n2, n3, n4, n5, n6, out
+):
+    nc = tc.nc
+    with ExitStack() as ctx:
+        keep = ctx.enter_context(tc.tile_pool(name="keep", bufs=1))
+        psum = ctx.enter_context(tc.psum_pool(name="psum", bufs=8))
+
+        def sb(shape, dtype, name):
+            return keep.tile(shape, dtype, name=name, align_bytes=64)
+
+        def load_list(src, name):
+            tile = sb([P, W // 16], U16, name)
+            nc.sync.dma_start(tile[:], src)
+            return tile
+
+        def half_of(lst, h):
+            return lst[:, h * (HALF // 16) : (h + 1) * (HALF // 16)]
+
+        def cols(h):
+            return slice(h * HALF, (h + 1) * HALF)
+
+        def mm(acc, lhs_w, lhs_s, rhs_w, rhs_s):
+            nc.tensor.matmul_mx(
+                out=acc, lhsT=lhs_w.bitcast(FP8X4), lhsT_scale=lhs_s, rhs=rhs_w.bitcast(FP8X4), rhs_scale=rhs_s,
+                start=True, stop=True,
+            )
+
+        ds_win = sb([P, G], U8, "ds_win")
+        xs_win = sb([P, T], U8, "xs_win")
+        nc.gpsimd.memset(ds_win[:].bitcast(I32), 0)
+        nc.gpsimd.memset(xs_win[:].bitcast(I32), 0)
+        warm = sb([P, 1], F32, "warm")
+        nc.vector.memset(warm[:], 0.0)
+        nc.scalar.activation(warm[:], warm[:], ACT.Sigmoid)
+        offs_l = load_list(offs, "offs_l")
+        xw_win = sb([P, T], U32, "xw_win")
+        nc.sync.dma_start(xw_win[:].bitcast(I32), x_words[0].rearrange("p n t -> p (n t)").bitcast(I32))
+        ds_rows = d_scales[0].bitcast(I32).rearrange("(g e) n -> e g n", e=2)
+        for e in range(2):
+            nc.scalar.dma_start(ds_win[:].bitcast(I32)[e:P:16, :], ds_rows[e])
+        two_l = load_list(two, "two_l")
+        k1_l = load_list(k1, "k1_l")
+        dw_win = sb([P, G], U32, "dw_win")
+        nc.sync.dma_start(dw_win[:].bitcast(I32), d_words[0].rearrange("p n t -> p (n t)").bitcast(I32))
+        for q in range(4):
+            nc.scalar.dma_start(xs_win[:].bitcast(I32)[32 * q : 32 * q + 4, :], x_scales[0].bitcast(I32)[4 * q : 4 * q + 4, :])
+        w_raw = sb([P, PACK, W], F32, "w_raw")
+        nc.sync.dma_start(w_raw[:], w1.rearrange("(p j) c -> p j c", j=PACK))
+        n1_l = load_list(n1, "n1_l")
+        n2_l = load_list(n2, "n2_l")
+        n3_l = load_list(n3, "n3_l")
+        n4_l = load_list(n4, "n4_l")
+        tab_rows = tab.rearrange("(p t) c -> t p c", t=PACK)
+        tab_win = [sb([P, W], F32, f"tab_win{t}") for t in range(PACK)]
+        for t in range(PACK):
+            nc.sync.dma_start(tab_win[t][:], tab_rows[t])
+        ga_t = sb([P, PACK], F32, "ga_t")
+        nc.sync.dma_start(ga_t[:], ga.rearrange("(p t) o -> p (t o)", t=PACK))
+        gb_t = sb([P, PACK], F32, "gb_t")
+        nc.sync.dma_start(gb_t[:], gb.rearrange("(p t) o -> p (t o)", t=PACK))
+        n5_l = load_list(n5, "n5_l")
+        n6_l = load_list(n6, "n6_l")
+        tab2_rows = tab2.rearrange("(p t) c -> t p c", t=PACK)
+        tab2_win = [sb([P, W], F32, f"tab2_win{t}") for t in range(PACK)]
+        for t in range(PACK):
+            nc.sync.dma_start(tab2_win[t][:], tab2_rows[t])
+
+        xq_w = sb([P, W], U32, "xq_w")
+        nc.vector.tensor_copy(xq_w[:], xw_win[:].indirect(offs_l[:]))
+        x2_w = sb([P, W], U32, "x2_w")
+        nc.vector.tensor_copy(x2_w[:], xw_win[:].indirect(two_l[:]))
+        ds_pick = sb([P, W], U8, "ds_pick")
+        nc.vector.tensor_copy(ds_pick[:], ds_win[:].indirect(k1_l[:]))
+        ds_deal = sb([P, PACK, P], U8, "ds_deal")
+        nc.vector.tensor_copy(ds_deal[:].rearrange("p t m -> p m t"), ds_pick[:].rearrange("p (m t) -> p m t", t=PACK))
+        ds_flat = ds_deal[:].rearrange("p t m -> p (t m)")
+        nc.scalar.dma_start(ds_flat.bitcast(I32)[2:P:32, :], ds_flat.bitcast(I32)[16:P:32, :])
+        nc.scalar.dma_start(ds_flat.bitcast(I32)[3:P:32, :], ds_flat.bitcast(I32)[17:P:32, :])
+        dw_pick = sb([P, W], U32, "dw_pick")
+        nc.vector.tensor_copy(dw_pick[:], dw_win[:].indirect(k1_l[:]))
+        dw_deal = sb([P, PACK, P], U32, "dw_deal")
+        nc.vector.tensor_copy(dw_deal[:].rearrange("p t m -> p m t"), dw_pick[:].rearrange("p (m t) -> p m t", t=PACK))
+        xq_s = sb([P, W], U8, "xq_s")
+        nc.vector.tensor_copy(xq_s[:], xs_win[:].indirect(offs_l[:]))
+        x2_s = sb([P, W], U8, "x2_s")
+        nc.vector.tensor_copy(x2_s[:], xs_win[:].indirect(two_l[:]))
+
+        w_il = sb([P, PACK, P, PACK], BF16, "w_il")
+        nc.scalar.copy(w_il[:].rearrange("p t m j -> p m j t"), w_raw[:].rearrange("p j (m t) -> p m j t", t=PACK))
+        w_w = sb([P, PACK, P], U32, "w_w")
+        w_s = sb([P, PACK, P], U8, "w_s")
+        nc.vector.quantize_mx(
+            out=w_w[:].rearrange("p t m -> p (t m)").bitcast(FP8X4),
+            scales=w_s[:].rearrange("p t m -> p (t m)"),
+            in_=w_il[:].rearrange("p t m j -> p (t m j)"),
+        )
+
+        a_win = [sb([P, W], F32, f"a_win{t}") for t in range(PACK)]
+        a_own = [sb([P, W], F32, f"a_own{t}") for t in range(PACK)]
+        for t in range(PACK):
+            acc = psum.tile([P, W], F32, name="acc")
+            mm(acc[:], dw_deal[:, t, :], ds_deal[:, t, :], xq_w[:], xq_s[:])
+            nc.scalar.activation(a_win[t][:], acc[:], ACT.Copy, scale=0.0625)
+            nc.scalar.activation(a_own[t][:], acc[:], ACT.Copy, scale=0.0625)
+        b_win = [sb([P, W], F32, f"b_win{t}") for t in range(PACK)]
+        for t in range(PACK):
+            acc = psum.tile([P, W], F32, name="acc")
+            mm(acc[:], w_w[:, t, :], w_s[:, t, :], x2_w[:], x2_s[:])
+            nc.scalar.copy(b_win[t][:], acc[:])
+        st_win = [sb([P, W], F32, f"st_win{t}") for t in range(PACK)]
+        gate = [sb([P, W], F32, f"gate{t}") for t in range(PACK)]
+        for t in range(PACK):
+            for h in range(2):
+                nc.vector.tensor_tensor(st_win[t][:, cols(h)], a_win[t][:].indirect(half_of(n1_l, h)), a_own[t][:, cols(h)], ALU.subtract)
+        for t in range(PACK):
+            for h in range(2):
+                nc.scalar.activation(gate[t][:, cols(h)], st_win[t][:].indirect(half_of(n2_l, h)), ACT.Sigmoid)
+
+        z2_il = [sb([P, HALF, PACK], BF16, f"z2_il{h}") for h in range(2)]
+        z2_w = [sb([P, HALF], U32, f"z2_w{h}") for h in range(2)]
+        z2_s = [sb([P, HALF], U8, f"z2_s{h}") for h in range(2)]
+
+        def z2_values(h):
+            rows = sb([P, PACK, HALF], BF16, f"z2_rows{h}")
+            for t in range(PACK):
+                first = sb([P, HALF], F32, f"first{h}{t}")
+                second = sb([P, HALF], F32, f"second{h}{t}")
+                larger = sb([P, HALF], F32, f"larger{h}{t}")
+                nc.vector.tensor_tensor(first[:], tab_win[t][:].indirect(half_of(n3_l, h)), b_win[t][:, cols(h)], ALU.add)
+                nc.vector.tensor_copy(second[:], b_win[t][:].indirect(half_of(n4_l, h)))
+                nc.vector.tensor_tensor(larger[:], first[:], second[:], ALU.max)
+                nc.scalar.activation(rows[:, t, :], larger[:], ACT.Copy, scale=gb_t[:, t : t + 1])
+            nc.scalar.copy(z2_il[h][:].rearrange("p (c i) t -> p c t i", i=4), rows[:].rearrange("p t (c i) -> p c t i", i=4))
+
+        def z2_quantize(h):
+            nc.vector.quantize_mx(out=z2_w[h][:].bitcast(FP8X4), scales=z2_s[h][:], in_=z2_il[h][:].rearrange("p c t -> p (c t)"))
+
+        z2_values(0)
+
+        z_rows = sb([P, PACK, W], BF16, "z_rows")
+        for t in range(PACK):
+            nc.vector.scalar_tensor_tensor(z_rows[:, t, :], a_own[t][:], ga_t[:, t : t + 1], gate[t][:], ALU.mult, ALU.mult)
+        z_il = sb([P, PACK, P, PACK], BF16, "z_il")
+        nc.scalar.copy(z_il[:].rearrange("p q m t -> p m t q"), z_rows[:].rearrange("p t (m q) -> p m t q", q=PACK))
+        z2_quantize(0)
+
+        z2_values(1)
+
+        z_w = sb([P, PACK, P], U32, "z_w")
+        z_s = sb([P, PACK, P], U8, "z_s")
+        nc.vector.quantize_mx(
+            out=z_w[:].rearrange("p q m -> p (q m)").bitcast(FP8X4),
+            scales=z_s[:].rearrange("p q m -> p (q m)"),
+            in_=z_il[:].rearrange("p q m t -> p (q m t)"),
+        )
+
+        s_own = [sb([P, W], F32, f"s_own{q}") for q in range(PACK)]
+        s_win = [sb([P, W], F32, f"s_win{q}") for q in range(PACK)]
+        prod = [sb([P, W], F32, f"prod{q}") for q in range(PACK)]
+
+        def s_product(q, h):
+            acc = psum.tile([P, W], F32, name="acc")
+            mm(acc[:, 0:HALF], z_w[:, q, :], z_s[:, q, :], z2_w[h][:], z2_s[h][:])
+            nc.scalar.activation(s_own[q][:, cols(h)], acc[:, 0:HALF], ACT.Copy, scale=0.0625)
+            nc.scalar.activation(s_win[q][:, cols(h)], acc[:, 0:HALF], ACT.Copy, scale=-0.03125)
+
+        def times_tab2(q, h):
+            nc.vector.tensor_tensor(prod[q][:, cols(h)], tab2_win[q][:].indirect(half_of(n5_l, h)), s_own[q][:, cols(h)], ALU.mult)
+
+        for q in range(PACK):
+            s_product(q, 0)
+        for q in range(PACK):
+            times_tab2(q, 0)
+        z2_quantize(1)
+        for q in range(PACK):
+            s_product(q, 1)
+        out_rows = out.rearrange("(p q) v -> q p v", q=PACK)
+        for q in range(PACK):
+            times_tab2(q, 1)
+            for h in range(2):
+                res = sb([P, HALF], F32, f"res{q}{h}")
+                nc.vector.tensor_tensor(res[:], s_win[q][:].indirect(half_of(n6_l, h)), prod[q][:, cols(h)], ALU.add)
+                nc.sync.dma_start(out_rows[q][:, cols(h)], res[:])

@@ -27,10 +27,10 @@ def tile_picked_ckqhopdkindkindg_none_p_kernel(
     nc = tc.nc
     with ExitStack() as ctx:
         keep = ctx.enter_context(tc.tile_pool(name="keep", bufs=1))
-        psum = ctx.enter_context(tc.psum_pool(name="psum", bufs=8))
+        psum = ctx.enter_context(tc.psum_pool(name="psum", bufs=4))
 
-        def sb(shape, dtype, name):
-            return keep.tile(shape, dtype, name=name, align_bytes=64)
+        def sb(shape, dtype, name, reuse=None):
+            return keep.tile(shape, dtype, name=name, tag=reuse or name, align_bytes=64)
 
         def load_list(src, name):
             tile = sb([P, W // 16], U16, name)
@@ -51,67 +51,59 @@ def tile_picked_ckqhopdkindkindg_none_p_kernel(
 
         ds_win = sb([P, G], U8, "ds_win")
         xs_win = sb([P, T], U8, "xs_win")
-        nc.gpsimd.memset(ds_win[:].bitcast(I32), 0)
+        nc.vector.memset(ds_win[:].bitcast(I32), 0)
         nc.gpsimd.memset(xs_win[:].bitcast(I32), 0)
-        warm = sb([P, 1], F32, "warm")
-        nc.vector.memset(warm[:], 0.0)
-        nc.scalar.activation(warm[:], warm[:], ACT.Sigmoid)
-        offs_l = load_list(offs, "offs_l")
         xw_win = sb([P, T], U32, "xw_win")
         nc.sync.dma_start(xw_win[:].bitcast(I32), x_words[0].rearrange("p n t -> p (n t)").bitcast(I32))
+        offs_l = load_list(offs, "offs_l")
+        k1_l = load_list(k1, "k1_l")
         ds_rows = d_scales[0].bitcast(I32).rearrange("(g e) n -> e g n", e=2)
         for e in range(2):
-            nc.scalar.dma_start(ds_win[:].bitcast(I32)[e:P:16, :], ds_rows[e])
-        two_l = load_list(two, "two_l")
-        k1_l = load_list(k1, "k1_l")
+            nc.sync.dma_start(ds_win[:].bitcast(I32)[e:P:16, :], ds_rows[e])
         dw_win = sb([P, G], U32, "dw_win")
         nc.sync.dma_start(dw_win[:].bitcast(I32), d_words[0].rearrange("p n t -> p (n t)").bitcast(I32))
-        for q in range(4):
-            nc.scalar.dma_start(xs_win[:].bitcast(I32)[32 * q : 32 * q + 4, :], x_scales[0].bitcast(I32)[4 * q : 4 * q + 4, :])
         w_raw = sb([P, PACK, W], F32, "w_raw")
         nc.sync.dma_start(w_raw[:], w1.rearrange("(p j) c -> p j c", j=PACK))
+        for q in range(4):
+            nc.sync.dma_start(xs_win[:].bitcast(I32)[32 * q : 32 * q + 4, :], x_scales[0].bitcast(I32)[4 * q : 4 * q + 4, :])
+        warm = sb([P, 1], F32, "warm")
+        nc.gpsimd.memset(warm[:], 0.0)
+        nc.scalar.activation(warm[:], warm[:], ACT.Sigmoid)
+        two_l = load_list(two, "two_l")
         n1_l = load_list(n1, "n1_l")
         n2_l = load_list(n2, "n2_l")
         n3_l = load_list(n3, "n3_l")
         n4_l = load_list(n4, "n4_l")
-        tab_rows = tab.rearrange("(p t) c -> t p c", t=PACK)
-        tab_win = [sb([P, W], F32, f"tab_win{t}") for t in range(PACK)]
-        for t in range(PACK):
-            nc.sync.dma_start(tab_win[t][:], tab_rows[t])
         ga_t = sb([P, PACK], F32, "ga_t")
         nc.sync.dma_start(ga_t[:], ga.rearrange("(p t) o -> p (t o)", t=PACK))
         gb_t = sb([P, PACK], F32, "gb_t")
         nc.sync.dma_start(gb_t[:], gb.rearrange("(p t) o -> p (t o)", t=PACK))
         n5_l = load_list(n5, "n5_l")
         n6_l = load_list(n6, "n6_l")
-        tab2_rows = tab2.rearrange("(p t) c -> t p c", t=PACK)
-        tab2_win = [sb([P, W], F32, f"tab2_win{t}") for t in range(PACK)]
-        for t in range(PACK):
-            nc.sync.dma_start(tab2_win[t][:], tab2_rows[t])
 
         xq_w = sb([P, W], U32, "xq_w")
         nc.vector.tensor_copy(xq_w[:], xw_win[:].indirect(offs_l[:]))
-        x2_w = sb([P, W], U32, "x2_w")
-        nc.vector.tensor_copy(x2_w[:], xw_win[:].indirect(two_l[:]))
         ds_pick = sb([P, W], U8, "ds_pick")
         nc.vector.tensor_copy(ds_pick[:], ds_win[:].indirect(k1_l[:]))
         ds_deal = sb([P, PACK, P], U8, "ds_deal")
-        nc.vector.tensor_copy(ds_deal[:].rearrange("p t m -> p m t"), ds_pick[:].rearrange("p (m t) -> p m t", t=PACK))
+        nc.vector.tensor_copy(ds_deal[:], ds_pick[:].rearrange("p (m t) -> p t m", t=PACK))
         ds_flat = ds_deal[:].rearrange("p t m -> p (t m)")
         nc.scalar.dma_start(ds_flat.bitcast(I32)[2:P:32, :], ds_flat.bitcast(I32)[16:P:32, :])
         nc.scalar.dma_start(ds_flat.bitcast(I32)[3:P:32, :], ds_flat.bitcast(I32)[17:P:32, :])
         dw_pick = sb([P, W], U32, "dw_pick")
         nc.vector.tensor_copy(dw_pick[:], dw_win[:].indirect(k1_l[:]))
-        dw_deal = sb([P, PACK, P], U32, "dw_deal")
-        nc.vector.tensor_copy(dw_deal[:].rearrange("p t m -> p m t"), dw_pick[:].rearrange("p (m t) -> p m t", t=PACK))
         xq_s = sb([P, W], U8, "xq_s")
         nc.vector.tensor_copy(xq_s[:], xs_win[:].indirect(offs_l[:]))
-        x2_s = sb([P, W], U8, "x2_s")
+        dw_deal = sb([P, PACK, P], U32, "dw_deal")
+        nc.vector.tensor_copy(dw_deal[:].rearrange("p t m -> p m t"), dw_pick[:].rearrange("p (m t) -> p m t", t=PACK))
+        x2_s = sb([P, W], U8, "x2_s", "dw_pick")
         nc.vector.tensor_copy(x2_s[:], xs_win[:].indirect(two_l[:]))
+        x2_w = sb([P, W], U32, "x2_w", "xs_win")
+        nc.vector.tensor_copy(x2_w[:], xw_win[:].indirect(two_l[:]))
 
-        w_il = sb([P, PACK, P, PACK], BF16, "w_il")
+        w_il = sb([P, PACK, P, PACK], BF16, "w_il", "ds_pick")
         nc.scalar.copy(w_il[:].rearrange("p t m j -> p m j t"), w_raw[:].rearrange("p j (m t) -> p m j t", t=PACK))
-        w_w = sb([P, PACK, P], U32, "w_w")
+        w_w = sb([P, PACK, P], U32, "w_w", "xw_win")
         w_s = sb([P, PACK, P], U8, "w_s")
         nc.vector.quantize_mx(
             out=w_w[:].rearrange("p t m -> p (t m)").bitcast(FP8X4),
@@ -119,13 +111,19 @@ def tile_picked_ckqhopdkindkindg_none_p_kernel(
             in_=w_il[:].rearrange("p t m j -> p (t m j)"),
         )
 
-        a_win = [sb([P, W], F32, f"a_win{t}") for t in range(PACK)]
+        a_win = [sb([P, W], F32, f"a_win{t}", "w_raw" if t == 0 else None) for t in range(PACK)]
         a_own = [sb([P, W], F32, f"a_own{t}") for t in range(PACK)]
         for t in range(PACK):
             acc = psum.tile([P, W], F32, name="acc")
             mm(acc[:], dw_deal[:, t, :], ds_deal[:, t, :], xq_w[:], xq_s[:])
             nc.scalar.activation(a_win[t][:], acc[:], ACT.Copy, scale=0.0625)
             nc.scalar.activation(a_own[t][:], acc[:], ACT.Copy, scale=0.0625)
+        tab_rows = tab.rearrange("(p t) c -> t p c", t=PACK)
+        dead = ["dw_win", "xq_w", "dw_deal", "ds_pick"]
+        tab_win = [sb([P, W], F32, f"tab_win{t}", dead[t]) for t in range(PACK)]
+        for t in range(PACK):
+            nc.sync.dma_start(tab_win[t][:], tab_rows[t])
+
         b_win = [sb([P, W], F32, f"b_win{t}") for t in range(PACK)]
         for t in range(PACK):
             acc = psum.tile([P, W], F32, name="acc")
@@ -140,35 +138,44 @@ def tile_picked_ckqhopdkindkindg_none_p_kernel(
             for h in range(2):
                 nc.scalar.activation(gate[t][:, cols(h)], st_win[t][:].indirect(half_of(n2_l, h)), ACT.Sigmoid)
 
+        tab2_rows = tab2.rearrange("(p t) c -> t p c", t=PACK)
+        tab2_win = [sb([P, W], F32, f"tab2_win{t}", f"st_win{t}") for t in range(PACK)]
+        for t in range(PACK):
+            nc.sync.dma_start(tab2_win[t][:], tab2_rows[t])
+
         z2_il = [sb([P, HALF, PACK], BF16, f"z2_il{h}") for h in range(2)]
         z2_w = [sb([P, HALF], U32, f"z2_w{h}") for h in range(2)]
         z2_s = [sb([P, HALF], U8, f"z2_s{h}") for h in range(2)]
 
-        def z2_values(h):
-            rows = sb([P, PACK, HALF], BF16, f"z2_rows{h}")
-            for t in range(PACK):
-                first = sb([P, HALF], F32, f"first{h}{t}")
-                second = sb([P, HALF], F32, f"second{h}{t}")
-                larger = sb([P, HALF], F32, f"larger{h}{t}")
-                nc.vector.tensor_tensor(first[:], tab_win[t][:].indirect(half_of(n3_l, h)), b_win[t][:, cols(h)], ALU.add)
-                nc.vector.tensor_copy(second[:], b_win[t][:].indirect(half_of(n4_l, h)))
-                nc.vector.tensor_tensor(larger[:], first[:], second[:], ALU.max)
-                nc.scalar.activation(rows[:, t, :], larger[:], ACT.Copy, scale=gb_t[:, t : t + 1])
-            nc.scalar.copy(z2_il[h][:].rearrange("p (c i) t -> p c t i", i=4), rows[:].rearrange("p t (c i) -> p c t i", i=4))
+        z2_rows = [sb([P, PACK, HALF], BF16, f"z2_rows{h}") for h in range(2)]
+
+        def z2_values(h, t, reuse=None):
+            first = sb([P, HALF], F32, f"first{h}{t}", reuse)
+            second = sb([P, HALF], F32, f"second{h}{t}", f"gate{t}" if h == 1 else None)
+            larger = sb([P, HALF], F32, f"larger{h}{t}")
+            nc.vector.tensor_tensor(first[:], tab_win[t][:].indirect(half_of(n3_l, h)), b_win[t][:, cols(h)], ALU.add)
+            nc.vector.tensor_copy(second[:], b_win[t][:].indirect(half_of(n4_l, h)))
+            nc.vector.tensor_tensor(larger[:], first[:], second[:], ALU.max)
+            nc.scalar.activation(z2_rows[h][:, t, :], larger[:], ACT.Copy, scale=gb_t[:, t : t + 1])
+
+        def z2_interleave(h):
+            nc.scalar.copy(z2_il[h][:].rearrange("p (c i) t -> p c t i", i=4), z2_rows[h][:].rearrange("p t (c i) -> p c t i", i=4))
 
         def z2_quantize(h):
             nc.vector.quantize_mx(out=z2_w[h][:].bitcast(FP8X4), scales=z2_s[h][:], in_=z2_il[h][:].rearrange("p c t -> p (c t)"))
 
-        z2_values(0)
+        for t in range(PACK):
+            z2_values(0, t)
+        z2_interleave(0)
 
         z_rows = sb([P, PACK, W], BF16, "z_rows")
         for t in range(PACK):
             nc.vector.scalar_tensor_tensor(z_rows[:, t, :], a_own[t][:], ga_t[:, t : t + 1], gate[t][:], ALU.mult, ALU.mult)
         z_il = sb([P, PACK, P, PACK], BF16, "z_il")
         nc.scalar.copy(z_il[:].rearrange("p q m t -> p m t q"), z_rows[:].rearrange("p t (m q) -> p m t q", q=PACK))
+        z2_values(1, 0)
         z2_quantize(0)
-
-        z2_values(1)
+        z2_values(1, 1, "z2_il0")
 
         z_w = sb([P, PACK, P], U32, "z_w")
         z_s = sb([P, PACK, P], U8, "z_s")
@@ -180,28 +187,46 @@ def tile_picked_ckqhopdkindkindg_none_p_kernel(
 
         s_own = [sb([P, W], F32, f"s_own{q}") for q in range(PACK)]
         s_win = [sb([P, W], F32, f"s_win{q}") for q in range(PACK)]
-        prod = [sb([P, W], F32, f"prod{q}") for q in range(PACK)]
+        prod = {}
 
-        def s_product(q, h):
-            acc = psum.tile([P, W], F32, name="acc")
-            mm(acc[:, 0:HALF], z_w[:, q, :], z_s[:, q, :], z2_w[h][:], z2_s[h][:])
-            nc.scalar.activation(s_own[q][:, cols(h)], acc[:, 0:HALF], ACT.Copy, scale=0.0625)
-            nc.scalar.activation(s_win[q][:, cols(h)], acc[:, 0:HALF], ACT.Copy, scale=-0.03125)
+        def s_product(h):
+            accs = []
+            for q in range(PACK):
+                acc = psum.tile([P, W], F32, name="acc" if h == 1 else "acc_early")
+                mm(acc[:, 0:HALF], z_w[:, q, :], z_s[:, q, :], z2_w[h][:], z2_s[h][:])
+                accs.append(acc)
+            return accs
 
-        def times_tab2(q, h):
-            nc.vector.tensor_tensor(prod[q][:, cols(h)], tab2_win[q][:].indirect(half_of(n5_l, h)), s_own[q][:, cols(h)], ALU.mult)
+        def s_plain(accs, q, h):
+            nc.scalar.activation(s_own[q][:, cols(h)], accs[q][:, 0:HALF], ACT.Copy, scale=0.0625)
 
+        def s_halved(accs, q, h):
+            nc.scalar.activation(s_win[q][:, cols(h)], accs[q][:, 0:HALF], ACT.Copy, scale=-0.03125)
+
+        def times_tab2(q, h, reuse=None):
+            prod[q, h] = sb([P, HALF], F32, f"prod{q}{h}", reuse)
+            nc.vector.tensor_tensor(prod[q, h][:], tab2_win[q][:].indirect(half_of(n5_l, h)), s_own[q][:, cols(h)], ALU.mult)
+
+        early = s_product(0)
         for q in range(PACK):
-            s_product(q, 0)
+            s_plain(early, q, 0)
+        z2_values(1, 2, "z_il")
+        z2_values(1, 3)
+        z2_interleave(1)
         for q in range(PACK):
+            s_halved(early, q, 0)
+        for q in range(PACK - 1):
             times_tab2(q, 0)
         z2_quantize(1)
-        for q in range(PACK):
-            s_product(q, 1)
+        times_tab2(PACK - 1, 0, "z2_il1")
+        late = s_product(1)
         out_rows = out.rearrange("(p q) v -> q p v", q=PACK)
+        for q in range(PACK):
+            s_plain(late, q, 1)
+            s_halved(late, q, 1)
         for q in range(PACK):
             times_tab2(q, 1)
             for h in range(2):
                 res = sb([P, HALF], F32, f"res{q}{h}")
-                nc.vector.tensor_tensor(res[:], s_win[q][:].indirect(half_of(n6_l, h)), prod[q][:, cols(h)], ALU.add)
+                nc.vector.tensor_tensor(res[:], s_win[q][:].indirect(half_of(n6_l, h)), prod[q, h][:], ALU.add)
                 nc.sync.dma_start(out_rows[q][:, cols(h)], res[:])

@@ -81,6 +81,14 @@ def tile_picked_ckqhopdkindkindg_none_p_kernel(
         n5_l = load_list(n5, "n5_l")
         n6_l = load_list(n6, "n6_l")
 
+        gb_sign = sb([P, PACK], F32, "gb_sign")
+        nc.gpsimd.tensor_scalar(gb_sign[:], gb_t[:], 0.0, 2.0, ALU.is_ge, ALU.mult)
+        nc.gpsimd.tensor_scalar(gb_sign[:], gb_sign[:], 1.0, -1.0, ALU.mult, ALU.add)
+        gb_size = sb([P, PACK], F32, "gb_size")
+        nc.gpsimd.tensor_tensor(gb_size[:], gb_t[:], gb_sign[:], ALU.mult)
+        ga_signed = sb([P, PACK], F32, "ga_signed")
+        nc.gpsimd.tensor_tensor(ga_signed[:], ga_t[:], gb_sign[:], ALU.mult)
+
         xq_w = sb([P, W], U32, "xq_w")
         nc.vector.tensor_copy(xq_w[:], xw_win[:].indirect(offs_l[:]))
         ds_pick = sb([P, W], U8, "ds_pick")
@@ -111,29 +119,33 @@ def tile_picked_ckqhopdkindkindg_none_p_kernel(
             in_=w_il[:].rearrange("p t m j -> p (t m j)"),
         )
 
-        a_win = [sb([P, W], F32, f"a_win{t}", "w_raw" if t == 0 else None) for t in range(PACK)]
-        a_own = [sb([P, W], F32, f"a_own{t}") for t in range(PACK)]
+        a_win = [sb([P, W if t == 0 else 2 * W], F32, f"a_win{t}", "w_raw" if t == 0 else None) for t in range(PACK)]
+        a_last = sb([P, W], F32, "a_last")
+        a_own = [a_win[t + 1][:, W : 2 * W] for t in range(PACK - 1)] + [a_last[:]]
         for t in range(PACK):
             acc = psum.tile([P, W], F32, name="acc")
             mm(acc[:], dw_deal[:, t, :], ds_deal[:, t, :], xq_w[:], xq_s[:])
-            nc.scalar.activation(a_win[t][:], acc[:], ACT.Copy, scale=0.0625)
-            nc.scalar.activation(a_own[t][:], acc[:], ACT.Copy, scale=0.0625)
+            nc.scalar.activation(a_win[t][:, 0:W], acc[:], ACT.Copy, scale=0.0625)
+            nc.scalar.activation(a_own[t], acc[:], ACT.Copy, scale=0.0625)
         tab_rows = tab.rearrange("(p t) c -> t p c", t=PACK)
         dead = ["dw_win", "xq_w", "dw_deal", "ds_pick"]
         tab_win = [sb([P, W], F32, f"tab_win{t}", dead[t]) for t in range(PACK)]
         for t in range(PACK):
             nc.sync.dma_start(tab_win[t][:], tab_rows[t])
 
+        b_own = [sb([P, W], F32, f"b_own{t}") for t in range(PACK)]
         b_win = [sb([P, W], F32, f"b_win{t}") for t in range(PACK)]
         for t in range(PACK):
             acc = psum.tile([P, W], F32, name="acc")
             mm(acc[:], w_w[:, t, :], w_s[:, t, :], x2_w[:], x2_s[:])
-            nc.scalar.copy(b_win[t][:], acc[:])
+            nc.scalar.copy(b_own[t][:], acc[:])
+            nc.scalar.activation(b_win[t][:], acc[:], ACT.Copy, scale=gb_size[:, t : t + 1])
         st_win = [sb([P, W], F32, f"st_win{t}") for t in range(PACK)]
         gate = [sb([P, W], F32, f"gate{t}") for t in range(PACK)]
-        for t in range(PACK):
-            for h in range(2):
-                nc.vector.tensor_tensor(st_win[t][:, cols(h)], a_win[t][:].indirect(half_of(n1_l, h)), a_own[t][:, cols(h)], ALU.subtract)
+        for h in range(2):
+            nc.vector.tensor_tensor(st_win[0][:, cols(h)], a_win[0][:].indirect(half_of(n1_l, h)), a_own[0][:, cols(h)], ALU.subtract)
+        for t in range(1, PACK):
+            nc.vector.tensor_tensor(st_win[t][:], a_win[t][:].indirect(n1_l[:]), a_own[t], ALU.subtract)
         for t in range(PACK):
             for h in range(2):
                 nc.scalar.activation(gate[t][:, cols(h)], st_win[t][:].indirect(half_of(n2_l, h)), ACT.Sigmoid)
@@ -149,14 +161,18 @@ def tile_picked_ckqhopdkindkindg_none_p_kernel(
 
         z2_rows = [sb([P, PACK, HALF], BF16, f"z2_rows{h}") for h in range(2)]
 
-        def z2_values(h, t, reuse=None):
+        pairs = {}
+
+        def z2_values(h, t, reuse=None, reuse_pair=None):
+            if t % 2 == 0:
+                pairs[h, t // 2] = (sb([P, 2, HALF], BF16, f"first_b{h}{t}"), sb([P, 2, HALF], BF16, f"second_b{h}{t}", reuse_pair))
+            first_b, second_b = pairs[h, t // 2]
             first = sb([P, HALF], F32, f"first{h}{t}", reuse)
-            second = sb([P, HALF], F32, f"second{h}{t}", f"gate{t}" if h == 1 else None)
-            larger = sb([P, HALF], F32, f"larger{h}{t}")
-            nc.vector.tensor_tensor(first[:], tab_win[t][:].indirect(half_of(n3_l, h)), b_win[t][:, cols(h)], ALU.add)
-            nc.vector.tensor_copy(second[:], b_win[t][:].indirect(half_of(n4_l, h)))
-            nc.vector.tensor_tensor(larger[:], first[:], second[:], ALU.max)
-            nc.scalar.activation(z2_rows[h][:, t, :], larger[:], ACT.Copy, scale=gb_t[:, t : t + 1])
+            nc.vector.tensor_tensor(first[:], tab_win[t][:].indirect(half_of(n3_l, h)), b_own[t][:, cols(h)], ALU.add)
+            nc.vector.tensor_copy(second_b[:, t % 2, :], b_win[t][:].indirect(half_of(n4_l, h)))
+            nc.scalar.activation(first_b[:, t % 2, :], first[:], ACT.Copy, scale=gb_size[:, t : t + 1])
+            if t % 2 == 1:
+                nc.vector.tensor_tensor(z2_rows[h][:, t - 1 : t + 1, :], first_b[:], second_b[:], ALU.max)
 
         def z2_interleave(h):
             nc.scalar.copy(z2_il[h][:].rearrange("p (c i) t -> p c t i", i=4), z2_rows[h][:].rearrange("p t (c i) -> p c t i", i=4))
@@ -170,13 +186,15 @@ def tile_picked_ckqhopdkindkindg_none_p_kernel(
 
         z_rows = sb([P, PACK, W], BF16, "z_rows")
         for t in range(PACK):
-            nc.vector.scalar_tensor_tensor(z_rows[:, t, :], a_own[t][:], ga_t[:, t : t + 1], gate[t][:], ALU.mult, ALU.mult)
+            nc.vector.scalar_tensor_tensor(z_rows[:, t, :], a_own[t], ga_signed[:, t : t + 1], gate[t][:], ALU.mult, ALU.mult)
         z_il = sb([P, PACK, P, PACK], BF16, "z_il")
         nc.scalar.copy(z_il[:].rearrange("p q m t -> p m t q"), z_rows[:].rearrange("p t (m q) -> p m t q", q=PACK))
         z2_values(1, 0)
+        z2_values(1, 1)
         z2_quantize(0)
-        z2_values(1, 1, "z2_il0")
+        z2_values(1, 2, "gate1", "gate3")
 
+        z2_values(1, 3, "gate2")
         z_w = sb([P, PACK, P], U32, "z_w")
         z_s = sb([P, PACK, P], U8, "z_s")
         nc.vector.quantize_mx(
@@ -185,8 +203,8 @@ def tile_picked_ckqhopdkindkindg_none_p_kernel(
             in_=z_il[:].rearrange("p q m t -> p (q m t)"),
         )
 
-        s_own = [sb([P, W], F32, f"s_own{q}") for q in range(PACK)]
-        s_win = [sb([P, W], F32, f"s_win{q}") for q in range(PACK)]
+        s_win = [sb([P, 2 * W], F32, f"s_win{q}") for q in range(PACK)]
+        s_own = [s_win[q][:, W : 2 * W] for q in range(PACK)]
         prod = {}
 
         def s_product(h):
@@ -204,21 +222,19 @@ def tile_picked_ckqhopdkindkindg_none_p_kernel(
             nc.scalar.activation(s_win[q][:, cols(h)], accs[q][:, 0:HALF], ACT.Copy, scale=-0.03125)
 
         def times_tab2(q, h, reuse=None):
-            prod[q, h] = sb([P, HALF], F32, f"prod{q}{h}", reuse)
-            nc.vector.tensor_tensor(prod[q, h][:], tab2_win[q][:].indirect(half_of(n5_l, h)), s_own[q][:, cols(h)], ALU.mult)
+            if h == 0:
+                prod[q] = sb([P, W], F32, f"prod{q}", reuse)
+            nc.vector.tensor_tensor(prod[q][:, cols(h)], tab2_win[q][:].indirect(half_of(n5_l, h)), s_own[q][:, cols(h)], ALU.mult)
 
         early = s_product(0)
-        for q in range(PACK):
-            s_plain(early, q, 0)
-        z2_values(1, 2, "z_il")
-        z2_values(1, 3)
         z2_interleave(1)
         for q in range(PACK):
+            s_plain(early, q, 0)
+        for q in range(PACK):
             s_halved(early, q, 0)
-        for q in range(PACK - 1):
-            times_tab2(q, 0)
         z2_quantize(1)
-        times_tab2(PACK - 1, 0, "z2_il1")
+        for q in range(PACK):
+            times_tab2(q, 0)
         late = s_product(1)
         out_rows = out.rearrange("(p q) v -> q p v", q=PACK)
         for q in range(PACK):
@@ -226,7 +242,11 @@ def tile_picked_ckqhopdkindkindg_none_p_kernel(
             s_halved(late, q, 1)
         for q in range(PACK):
             times_tab2(q, 1)
-            for h in range(2):
-                res = sb([P, HALF], F32, f"res{q}{h}")
-                nc.vector.tensor_tensor(res[:], s_win[q][:].indirect(half_of(n6_l, h)), prod[q, h][:], ALU.add)
-                nc.sync.dma_start(out_rows[q][:, cols(h)], res[:])
+            res = sb([P, W], F32, f"res{q}")
+            if q < PACK - 1:
+                nc.vector.tensor_tensor(res[:], s_win[q][:].indirect(n6_l[:]), prod[q][:], ALU.add)
+                nc.sync.dma_start(out_rows[q], res[:])
+            else:
+                for h in range(2):
+                    nc.vector.tensor_tensor(res[:, cols(h)], s_win[q][:].indirect(half_of(n6_l, h)), prod[q][:, cols(h)], ALU.add)
+                    nc.sync.dma_start(out_rows[q][:, cols(h)], res[:, cols(h)])

@@ -88,6 +88,7 @@ def tile_picked_ckqhopdkindkindg_none_p_kernel(
         nc.gpsimd.tensor_tensor(gb_size[:], gb_t[:], gb_sign[:], ALU.mult)
         ga_signed = sb([P, PACK], F32, "ga_signed")
         nc.gpsimd.tensor_tensor(ga_signed[:], ga_t[:], gb_sign[:], ALU.mult)
+        nc.gpsimd.tensor_scalar(ga_signed[:], ga_signed[:], 0.0625, 0.0, ALU.mult, ALU.add)
 
         xq_w = sb([P, W], U32, "xq_w")
         nc.vector.tensor_copy(xq_w[:], xw_win[:].indirect(offs_l[:]))
@@ -122,8 +123,10 @@ def tile_picked_ckqhopdkindkindg_none_p_kernel(
         a_win = [sb([P, W if t == 0 else 2 * W], F32, f"a_win{t}", "w_raw" if t == 0 else None) for t in range(PACK)]
         a_last = sb([P, W], F32, "a_last")
         a_own = [a_win[t + 1][:, W : 2 * W] for t in range(PACK - 1)] + [a_last[:]]
+        a_sum = []
         for t in range(PACK):
             acc = psum.tile([P, W], F32, name="acc")
+            a_sum.append(acc)
             mm(acc[:], dw_deal[:, t, :], ds_deal[:, t, :], xq_w[:], xq_s[:])
             nc.scalar.activation(a_win[t][:, 0:W], acc[:], ACT.Copy, scale=0.0625)
             nc.scalar.activation(a_own[t], acc[:], ACT.Copy, scale=0.0625)
@@ -136,7 +139,7 @@ def tile_picked_ckqhopdkindkindg_none_p_kernel(
         b_own = [sb([P, W], F32, f"b_own{t}") for t in range(PACK)]
         b_win = [sb([P, W], F32, f"b_win{t}") for t in range(PACK)]
         for t in range(PACK):
-            acc = psum.tile([P, W], F32, name="acc")
+            acc = psum.tile([P, W], F32, name="acc_early")
             mm(acc[:], w_w[:, t, :], w_s[:, t, :], x2_w[:], x2_s[:])
             nc.scalar.copy(b_own[t][:], acc[:])
             nc.scalar.activation(b_win[t][:], acc[:], ACT.Copy, scale=gb_size[:, t : t + 1])
@@ -186,7 +189,7 @@ def tile_picked_ckqhopdkindkindg_none_p_kernel(
 
         z_rows = sb([P, PACK, W], BF16, "z_rows")
         for t in range(PACK):
-            nc.vector.scalar_tensor_tensor(z_rows[:, t, :], a_own[t], ga_signed[:, t : t + 1], gate[t][:], ALU.mult, ALU.mult)
+            nc.vector.scalar_tensor_tensor(z_rows[:, t, :], a_sum[t][:], ga_signed[:, t : t + 1], gate[t][:], ALU.mult, ALU.mult)
         z_il = sb([P, PACK, P, PACK], BF16, "z_il")
         nc.scalar.copy(z_il[:].rearrange("p q m t -> p m t q"), z_rows[:].rearrange("p t (m q) -> p m t q", q=PACK))
         z2_values(1, 0)

from contextlib import ExitStack

import concourse.mybir as mybir

F32 = mybir.dt.float32
BF16 = mybir.dt.bfloat16
I32 = mybir.dt.int32
U32 = mybir.dt.uint32
U16 = mybir.dt.uint16
U8 = mybir.dt.uint8
FP8X4 = mybir.dt.float8_e4m3fn_x4
ALU = mybir.AluOpType
ACT = mybir.ActivationFunctionType

P = 128
PACK = 4
W = 512
HALF = 256
T = 1024
G = 2048
FLOPS = 3 * 2 * 512 * 512 * 512


def tile_picked_ckqhopdkindkindg_none_p_kernel(
    tc, x_words, x_scales, d_words, d_scales, w1, tab, ga, gb, tab2, offs, k1, two, n1, n2, n3, n4, n5, n6, out
):
    nc = tc.nc
    with ExitStack() as ctx:
        keep = ctx.enter_context(tc.tile_pool(name="keep", bufs=1))
        psum = ctx.enter_context(tc.psum_pool(name="psum", bufs=4))

        def sb(shape, dtype, name, reuse=None):
            return keep.tile(shape, dtype, name=name, tag=reuse or name, align_bytes=64)

        def load_list(src, name):
            tile = sb([P, W // 16], U16, name)
            nc.sync.dma_start(tile[:], src)
            return tile

        def half_of(lst, h):
            return lst[:, h * (HALF // 16) : (h + 1) * (HALF // 16)]

        def cols(h):
            return slice(h * HALF, (h + 1) * HALF)

        def mm(acc, lhs_w, lhs_s, rhs_w, rhs_s):
            nc.tensor.matmul_mx(
                out=acc, lhsT=lhs_w.bitcast(FP8X4), lhsT_scale=lhs_s, rhs=rhs_w.bitcast(FP8X4), rhs_scale=rhs_s,
                start=True, stop=True,
            )

        ds_win = sb([P, G], U8, "ds_win")
        xs_win = sb([P, T], U8, "xs_win")
        nc.vector.memset(ds_win[:].bitcast(I32), 0)
        nc.gpsimd.memset(xs_win[:].bitcast(I32), 0)
        xw_win = sb([P, T], U32, "xw_win")
        nc.sync.dma_start(xw_win[:].bitcast(I32), x_words[0].rearrange("p n t -> p (n t)").bitcast(I32))
        offs_l = load_list(offs, "offs_l")
        k1_l = load_list(k1, "k1_l")
        ds_rows = d_scales[0].bitcast(I32).rearrange("(g e) n -> e g n", e=2)
        for e in range(2):
            nc.sync.dma_start(ds_win[:].bitcast(I32)[e:P:16, :], ds_rows[e])
        dw_win = sb([P, G], U32, "dw_win")
        nc.sync.dma_start(dw_win[:].bitcast(I32), d_words[0].rearrange("p n t -> p (n t)").bitcast(I32))
        w_raw = sb([P, PACK, W], F32, "w_raw")
        nc.sync.dma_start(w_raw[:], w1.rearrange("(p j) c -> p j c", j=PACK))
        for q in range(4):
            nc.sync.dma_start(xs_win[:].bitcast(I32)[32 * q : 32 * q + 4, :], x_scales[0].bitcast(I32)[4 * q : 4 * q + 4, :])
        warm = sb([P, 1], F32, "warm")
        nc.gpsimd.memset(warm[:], 0.0)
        nc.scalar.activation(warm[:], warm[:], ACT.Sigmoid)
        two_l = load_list(two, "two_l")
        n1_l = load_list(n1, "n1_l")
        n2_l = load_list(n2, "n2_l")
        n3_l = load_list(n3, "n3_l")
        n4_l = load_list(n4, "n4_l")
        ga_t = sb([P, PACK], F32, "ga_t")
        nc.sync.dma_start(ga_t[:], ga.rearrange("(p t) o -> p (t o)", t=PACK))
        gb_t = sb([P, PACK], F32, "gb_t")
        nc.sync.dma_start(gb_t[:], gb.rearrange("(p t) o -> p (t o)", t=PACK))
        n5_l = load_list(n5, "n5_l")
        n6_l = load_list(n6, "n6_l")

        gb_sign = sb([P, PACK], F32, "gb_sign")
        nc.gpsimd.tensor_scalar(gb_sign[:], gb_t[:], 0.0, 2.0, ALU.is_ge, ALU.mult)
        nc.gpsimd.tensor_scalar(gb_sign[:], gb_sign[:], 1.0, -1.0, ALU.mult, ALU.add)
        gb_size = sb([P, PACK], F32, "gb_size")
        nc.gpsimd.tensor_tensor(gb_size[:], gb_t[:], gb_sign[:], ALU.mult)
        ga_signed = sb([P, PACK], F32, "ga_signed")
        nc.gpsimd.tensor_tensor(ga_signed[:], ga_t[:], gb_sign[:], ALU.mult)
        nc.gpsimd.tensor_scalar(ga_signed[:], ga_signed[:], 0.0625, 0.0, ALU.mult, ALU.add)

        xq_w = sb([P, W], U32, "xq_w")
        nc.vector.tensor_copy(xq_w[:], xw_win[:].indirect(offs_l[:]))
        ds_pick = sb([P, W], U8, "ds_pick")
        nc.vector.tensor_copy(ds_pick[:], ds_win[:].indirect(k1_l[:]))
        ds_deal = sb([P, PACK, P], U8, "ds_deal")
        nc.vector.tensor_copy(ds_deal[:], ds_pick[:].rearrange("p (m t) -> p t m", t=PACK))
        ds_flat = ds_deal[:].rearrange("p t m -> p (t m)")
        nc.scalar.dma_start(ds_flat.bitcast(I32)[2:P:32, :], ds_flat.bitcast(I32)[16:P:32, :])
        nc.scalar.dma_start(ds_flat.bitcast(I32)[3:P:32, :], ds_flat.bitcast(I32)[17:P:32, :])
        dw_pick = sb([P, W], U32, "dw_pick")
        nc.vector.tensor_copy(dw_pick[:], dw_win[:].indirect(k1_l[:]))
        xq_s = sb([P, W], U8, "xq_s")
        nc.vector.tensor_copy(xq_s[:], xs_win[:].indirect(offs_l[:]))
        dw_deal = sb([P, PACK, P], U32, "dw_deal")
        nc.vector.tensor_copy(dw_deal[:].rearrange("p t m -> p m t"), dw_pick[:].rearrange("p (m t) -> p m t", t=PACK))
        x2_s = sb([P, W], U8, "x2_s", "dw_pick")
        nc.vector.tensor_copy(x2_s[:], xs_win[:].indirect(two_l[:]))
        x2_w = sb([P, W], U32, "x2_w", "xs_win")
        nc.vector.tensor_copy(x2_w[:], xw_win[:].indirect(two_l[:]))

        w_il = sb([P, PACK, P, PACK], BF16, "w_il", "ds_pick")
        nc.scalar.copy(w_il[:].rearrange("p t m j -> p m j t"), w_raw[:].rearrange("p j (m t) -> p m j t", t=PACK))
        w_w = sb([P, PACK, P], U32, "w_w", "xw_win")
        w_s = sb([P, PACK, P], U8, "w_s")
        nc.vector.quantize_mx(
            out=w_w[:].rearrange("p t m -> p (t m)").bitcast(FP8X4),
            scales=w_s[:].rearrange("p t m -> p (t m)"),
            in_=w_il[:].rearrange("p t m j -> p (t m j)"),
        )

        a_win = [sb([P, W if t == 0 else 2 * W], F32, f"a_win{t}", "w_raw" if t == 0 else None) for t in range(PACK)]
        a_last = sb([P, W], F32, "a_last")
        a_own = [a_win[t + 1][:, W : 2 * W] for t in range(PACK - 1)] + [a_last[:]]
        a_sum = []
        for t in range(PACK):
            acc = psum.tile([P, W], F32, name="acc")
            a_sum.append(acc)
            mm(acc[:], dw_deal[:, t, :], ds_deal[:, t, :], xq_w[:], xq_s[:])
            nc.scalar.activation(a_win[t][:, 0:W], acc[:], ACT.Copy, scale=0.0625)
            nc.scalar.activation(a_own[t], acc[:], ACT.Copy, scale=0.0625)
        tab_rows = tab.rearrange("(p t) c -> t p c", t=PACK)
        dead = ["dw_win", "xq_w", "dw_deal", "ds_pick"]
        tab_win = [sb([P, W], F32, f"tab_win{t}", dead[t]) for t in range(PACK)]
        for t in range(PACK):
            nc.sync.dma_start(tab_win[t][:], tab_rows[t])

        b_own = [sb([P, W], F32, f"b_own{t}") for t in range(PACK)]
        b_win = [sb([P, W], F32, f"b_win{t}") for t in range(PACK)]
        for t in range(PACK):
            acc = psum.tile([P, W], F32, name="acc_early")
            mm(acc[:], w_w[:, t, :], w_s[:, t, :], x2_w[:], x2_s[:])
            nc.scalar.copy(b_own[t][:], acc[:])
            nc.scalar.activation(b_win[t][:], acc[:], ACT.Copy, scale=gb_size[:, t : t + 1])
        st_win = [sb([P, W], F32, f"st_win{t}") for t in range(PACK)]
        gate = [sb([P, W], F32, f"gate{t}") for t in range(PACK)]
        for h in range(2):
            nc.vector.tensor_tensor(st_win[0][:, cols(h)], a_win[0][:].indirect(half_of(n1_l, h)), a_own[0][:, cols(h)], ALU.subtract)
        for t in range(1, PACK):
            nc.vector.tensor_tensor(st_win[t][:], a_win[t][:].indirect(n1_l[:]), a_own[t], ALU.subtract)
        for t in range(PACK):
            for h in range(2):
                nc.scalar.activation(gate[t][:, cols(h)], st_win[t][:].indirect(half_of(n2_l, h)), ACT.Sigmoid)

        tab2_rows = tab2.rearrange("(p t) c -> t p c", t=PACK)
        tab2_win = [sb([P, W], F32, f"tab2_win{t}", f"st_win{t}") for t in range(PACK)]
        for t in range(PACK):
            nc.sync.dma_start(tab2_win[t][:], tab2_rows[t])

        z2_il = [sb([P, HALF, PACK], BF16, f"z2_il{h}") for h in range(2)]
        z2_w = [sb([P, HALF], U32, f"z2_w{h}") for h in range(2)]
        z2_s = [sb([P, HALF], U8, f"z2_s{h}") for h in range(2)]

        z2_rows = [sb([P, PACK, HALF], BF16, f"z2_rows{h}") for h in range(2)]

        pairs = {}

        def z2_values(h, t, reuse=None, reuse_pair=None):
            if t % 2 == 0:
                pairs[h, t // 2] = (sb([P, 2, HALF], BF16, f"first_b{h}{t}"), sb([P, 2, HALF], BF16, f"second_b{h}{t}", reuse_pair))
            first_b, second_b = pairs[h, t // 2]
            first = sb([P, HALF], F32, f"first{h}{t}", reuse)
            nc.vector.tensor_tensor(first[:], tab_win[t][:].indirect(half_of(n3_l, h)), b_own[t][:, cols(h)], ALU.add)
            nc.vector.tensor_copy(second_b[:, t % 2, :], b_win[t][:].indirect(half_of(n4_l, h)))
            nc.scalar.activation(first_b[:, t % 2, :], first[:], ACT.Copy, scale=gb_size[:, t : t + 1])
            if t % 2 == 1:
                nc.vector.tensor_tensor(z2_rows[h][:, t - 1 : t + 1, :], first_b[:], second_b[:], ALU.max)

        def z2_interleave(h):
            nc.scalar.copy(z2_il[h][:].rearrange("p (c i) t -> p c t i", i=4), z2_rows[h][:].rearrange("p t (c i) -> p c t i", i=4))

        def z2_quantize(h):
            nc.vector.quantize_mx(out=z2_w[h][:].bitcast(FP8X4), scales=z2_s[h][:], in_=z2_il[h][:].rearrange("p c t -> p (c t)"))

        for t in range(PACK):
            z2_values(0, t)
        z2_interleave(0)

        z_rows = sb([P, PACK, W], BF16, "z_rows")
        for t in range(PACK):
            nc.vector.scalar_tensor_tensor(z_rows[:, t, :], a_sum[t][:], ga_signed[:, t : t + 1], gate[t][:], ALU.mult, ALU.mult)
        z_il = sb([P, PACK, P, PACK], BF16, "z_il")
        nc.scalar.copy(z_il[:].rearrange("p q m t -> p m t q"), z_rows[:].rearrange("p t (m q) -> p m t q", q=PACK))
        z2_values(1, 0)
        z2_values(1, 1)
        z2_quantize(0)
        z2_values(1, 2, "gate1", "gate3")

        z2_values(1, 3, "gate2")
        z_w = sb([P, PACK, P], U32, "z_w")
        z_s = sb([P, PACK, P], U8, "z_s")
        nc.vector.quantize_mx(
            out=z_w[:].rearrange("p q m -> p (q m)").bitcast(FP8X4),
            scales=z_s[:].rearrange("p q m -> p (q m)"),
            in_=z_il[:].rearrange("p q m t -> p (q m t)"),
        )

        s_win = [sb([P, 2 * W], F32, f"s_win{q}") for q in range(PACK)]
        s_own = [s_win[q][:, W : 2 * W] for q in range(PACK)]
        prod = {}

        def s_product(h):
            accs = []
            for q in range(PACK):
                acc = psum.tile([P, W], F32, name="acc" if h == 1 else "acc_early")
                mm(acc[:, 0:HALF], z_w[:, q, :], z_s[:, q, :], z2_w[h][:], z2_s[h][:])
                accs.append(acc)
            return accs

        def s_plain(accs, q, h):
            nc.scalar.activation(s_own[q][:, cols(h)], accs[q][:, 0:HALF], ACT.Copy, scale=0.0625)

        def s_halved(accs, q, h):
            nc.scalar.activation(s_win[q][:, cols(h)], accs[q][:, 0:HALF], ACT.Copy, scale=-0.03125)

        def times_tab2(q, h, reuse=None):
            if h == 0:
                prod[q] = sb([P, W], F32, f"prod{q}", reuse)
            nc.vector.tensor_tensor(prod[q][:, cols(h)], tab2_win[q][:].indirect(half_of(n5_l, h)), s_own[q][:, cols(h)], ALU.mult)

        early = s_product(0)
        z2_interleave(1)
        for q in range(PACK):
            s_plain(early, q, 0)
        for q in range(PACK):
            s_halved(early, q, 0)
        z2_quantize(1)
        for q in range(PACK):
            times_tab2(q, 0)
        late = s_product(1)
        out_rows = out.rearrange("(p q) v -> q p v", q=PACK)
        for q in range(PACK):
            s_plain(late, q, 1)
            s_halved(late, q, 1)
        for q in range(PACK):
            times_tab2(q, 1)
            res = sb([P, W], F32, f"res{q}")
            if q < PACK - 1:
                nc.vector.tensor_tensor(res[:], s_win[q][:].indirect(n6_l[:]), prod[q][:], ALU.add)
                nc.sync.dma_start(out_rows[q], res[:])
            else:
                for h in range(2):
                    nc.vector.tensor_tensor(res[:, cols(h)], s_win[q][:].indirect(half_of(n6_l, h)), prod[q][:, cols(h)], ALU.add)
                    nc.sync.dma_start(out_rows[q][:, cols(h)], res[:, cols(h)])
